import numpy as np
import ml_dtypes


def mxq(x, axis, fmt="e4m3"):
    dtype, down = {"e4m3": (ml_dtypes.float8_e4m3fn, 7), "e5m2": (ml_dtypes.float8_e5m2, 14)}[fmt]
    v = np.moveaxis(np.asarray(x, np.float32).astype(ml_dtypes.bfloat16).astype(np.float64), axis, -1)
    blocks = v.reshape(v.shape[:-1] + (-1, 32))
    amax = np.abs(blocks).max(-1, keepdims=True)
    byte = np.maximum(np.where(amax > 0, np.frexp(amax)[1] - 1 + 127, 0) - down, 1)
    scale = np.exp2(byte - 127.0)
    codes = (blocks / scale).astype(np.float32).astype(dtype).astype(np.float64)
    return np.moveaxis((codes * scale).reshape(v.shape), -1, axis)


WIDE = False


def mx_kscale(k):
    if not WIDE:
        return np.ones(k)
    levels = np.array([10, -10, 5, -5, 0])
    if k % 512:
        return np.exp2(np.random.permutation(np.resize(levels, k // 32))).repeat(32)
    a = np.empty((k // 512, 16))
    for p in range(k // 512):
        a[p, :8] = np.random.permutation(np.resize(levels, 8))
        for g in range(8):
            far = levels[np.abs(levels - a[p, g]) >= 10]
            a[p, g + 8] = far[np.random.randint(len(far))]
    return np.exp2(a.ravel()).repeat(32)


def f64(x):
    return np.asarray(x).astype(np.float64)


def striped(idx):
    return np.tile(idx.reshape(-1, 16).T, (8, 1)).astype(np.uint16)


def unstriped(offs):
    return offs[:16].T.reshape(-1).astype(np.int64)


def striped8(idx):
    return np.concatenate([x.reshape(-1, 16).T for x in idx]).astype(np.uint16)


def runs(offs, k):
    lists = np.stack([offs[16 * r : 16 * r + 16].T.reshape(-1) for r in range(8)]).astype(np.int64)
    return lists[np.arange(k) % 512 // 64]


def pack_weight(w):
    k, n = w.shape
    w = f64(np.asarray(w, np.float32).astype(ml_dtypes.bfloat16)).reshape(k // 32, 32, n)
    amax = np.abs(w).max(1)
    byte = np.clip(np.where(amax > 0, np.frexp(amax)[1] - 1 + 127 - 7, 1), 1, 254)
    scaled = (w * np.exp2(127.0 - byte)[:, None, :]).reshape(k, n).astype(np.float32)
    words = np.ascontiguousarray(scaled.reshape(k // 512, 128, 4, n).transpose(0, 1, 3, 2)).astype(ml_dtypes.float8_e4m3fn).view(np.uint8)
    return words, np.ascontiguousarray(byte.astype(np.uint8).reshape(k // 512, 16, n))


def unpack_weight(words, scales):
    g, p, n, _ = words.shape
    vals = np.ascontiguousarray(words).view(ml_dtypes.float8_e4m3fn).astype(np.float64) * np.repeat(np.exp2(scales.astype(np.float64) - 127.0), 8, axis=1)[..., None]
    return vals.transpose(0, 1, 3, 2).reshape(g * 512, n)


def relu(v):
    return np.maximum(v, 0.0)


def sigmoid(v):
    return 1.0 / (1.0 + np.exp(-np.maximum(v, -700.0)))


K, T, S, N, G, H = 512, 2048, 256, 512, 2048, 512


def setup_inputs():
    n = np.random.standard_normal
    s = mx_kscale(K)[:, None]
    u = mx_kscale(K)
    packed_xT = pack_weight(n((K, T)) * s)
    packed_dT = pack_weight(n((K, G)) / s)
    return {
        "x_words": packed_xT[0],
        "x_scales": packed_xT[1],
        "d_words": packed_dT[0],
        "d_scales": packed_dT[1],
        "sl": np.random.uniform(1.0, 2.0, (H, 1)).astype(np.float32),
        "th": (0.5 * n((H, 1))).astype(np.float32),
        "gn": (np.random.uniform(0.5, 1.5, (H, 1)) * u[:, None]).astype(np.float32),
        "w1": (n((H, N)) / np.sqrt(H) / u[:, None]).astype(np.float32),
        "offs": striped(np.random.permutation(T)[:S]),
        "ci": striped(np.random.permutation(G)[:H]),
        "n1": striped8(np.stack([np.random.permutation(S) for _ in range(8)])),
        "n2": striped8(np.stack([np.random.permutation(S) for _ in range(8)])),
        "n3": striped(np.random.permutation(S)),
    }


def reference(x_words, x_scales, d_words, d_scales, sl, th, gn, w1, offs, ci, n1, n2, n3):
    d_ci = unpack_weight(d_words, d_scales)[:, unstriped(ci)]
    xq = unpack_weight(x_words, x_scales)[:, unstriped(offs)]
    s = 0.0625 * (d_ci.T @ xq)
    st = np.maximum(s, s[np.arange(H)[:, None], runs(n1, H)])
    sg = sigmoid(f64(sl) * (st[np.arange(H)[:, None], runs(n2, H)] - f64(th)))
    z = f64(gn) * (st * sg)
    h = mxq(f64(w1), 0, "e4m3").T @ mxq(z, 0, "e4m3")
    rl = relu(h)
    ds = np.zeros((N, S))
    ds[:, unstriped(n3)] = rl
    return ds - (0.5 * h)

@@ -1,0 +1,200 @@
+from contextlib import ExitStack
+
+import concourse.mybir as mybir
+
+K, T, S, N, G, H = 512, 2048, 256, 512, 2048, 512
+FLOPS = 2 * K * H * S + 2 * H * N * S
+
+F32 = mybir.dt.float32
+BF16 = mybir.dt.bfloat16
+I32 = mybir.dt.int32
+U32 = mybir.dt.uint32
+U16 = mybir.dt.uint16
+U8 = mybir.dt.uint8
+FP8X4 = mybir.dt.float8_e4m3fn_x4
+ALU = mybir.AluOpType
+ACT = mybir.ActivationFunctionType
+
+P = 128
+PACK = 4
+LIST_ROWS = 16
+X_PLANE_ROW = 4
+M_TILES = N // P
+CHUNKS = ((0, 64), (64, 128), (128, 256))
+
+
+def list_slice(offsets, lo, hi):
+    return offsets[:, lo // LIST_ROWS : hi // LIST_ROWS]
+
+
+def tile_picked_dwlehhsend_none_p_kernel(
+    tc, x_words, x_scales, d_words, d_scales, sl, th, gn, w1, offs, ci, n1, n2, n3, out
+):
+    nc = tc.nc
+    with ExitStack() as ctx:
+        keep = ctx.enter_context(tc.tile_pool(name="keep", bufs=1))
+        psum = ctx.enter_context(tc.psum_pool(name="psum", bufs=1))
+
+        def sbuf(shape, dtype, name, slot=None):
+            return keep.tile(shape, dtype, name=name, tag=slot or name, align_bytes=64)
+
+        ci_l = sbuf([P, H // LIST_ROWS], U16, "ci_l")
+        offs_l = sbuf([P, S // LIST_ROWS], U16, "offs_l")
+        n1_l = sbuf([P, S // LIST_ROWS], U16, "n1_l")
+        n2_l = sbuf([P, S // LIST_ROWS], U16, "n2_l")
+        n3_l = sbuf([P, S // LIST_ROWS], U16, "n3_l")
+        d_tab = sbuf([P, G], I32, "d_tab")
+        x_tab = sbuf([P, T], I32, "x_tab")
+        d_tab_sc = sbuf([P, G], U8, "d_tab_sc")
+        x_tab_sc = sbuf([P, T], U8, "x_tab_sc")
+        w_raw = sbuf([P, PACK, N], F32, "w_raw")
+        sl_t = sbuf([P, PACK], F32, "sl_t")
+        th_t = sbuf([P, PACK], F32, "th_t")
+        gn_t = sbuf([P, PACK], F32, "gn_t")
+
+        nc.vector.memset(d_tab_sc[:].bitcast(I32), 0)
+        nc.vector.memset(x_tab_sc[:].bitcast(I32), 0)
+
+        def load_scales(eng, tab_sc, scales, row0, quads):
+            for q in quads:
+                eng.dma_start(
+                    out=tab_sc[32 * q + row0 : 32 * q + row0 + 4, :].bitcast(I32),
+                    in_=scales[0, 4 * q : 4 * q + 4, :].bitcast(I32),
+                )
+
+        def words(dram):
+            return dram[0].rearrange("p c r -> p (c r)").bitcast(I32)
+
+        load_scales(nc.scalar, d_tab_sc, d_scales, 0, range(4))
+        load_scales(nc.scalar, x_tab_sc, x_scales, X_PLANE_ROW, range(4))
+        nc.sync.dma_start(ci_l[:], ci)
+        nc.sync.dma_start(offs_l[:], offs)
+        nc.sync.dma_start(out=d_tab[:], in_=words(d_words))
+        nc.sync.dma_start(out=x_tab[:], in_=words(x_words))
+        nc.sync.dma_start(n1_l[:], n1)
+        nc.sync.dma_start(n2_l[:], n2)
+        nc.sync.dma_start(out=w_raw[:], in_=w1.rearrange("(p t) n -> p t n", t=PACK))
+        for col, dram in ((sl_t, sl), (th_t, th), (gn_t, gn)):
+            nc.sync.dma_start(out=col[:], in_=dram.rearrange("(p t) o -> p (t o)", t=PACK))
+        nc.sync.dma_start(n3_l[:], n3)
+
+        d_codes = sbuf([P, H], U32, "d_codes")
+        d_sc = sbuf([P, H], U8, "d_sc")
+        x_codes = sbuf([P, S], U32, "x_codes")
+        x_sc = sbuf([P, S], U8, "x_sc")
+        nc.vector.tensor_copy(d_sc[:].rearrange("p (t m) -> p m t", t=PACK), d_tab_sc[:].indirect(ci_l[:]))
+        nc.vector.tensor_copy(x_sc[:], x_tab_sc[:].indirect(offs_l[:]))
+        nc.vector.tensor_copy(d_codes[:].rearrange("p (t m) -> p m t", t=PACK), d_tab[:].bitcast(U32).indirect(ci_l[:]))
+        nc.vector.tensor_copy(x_codes[:], x_tab[:].bitcast(U32).indirect(offs_l[:]))
+
+        s_sb = [sbuf([P, S], F32, f"s_sb{t}") for t in range(PACK)]
+        s_n1 = [sbuf([P, S], F32, f"s_n1{t}") for t in range(PACK)]
+        st = [sbuf([P, S], F32, f"st{t}") for t in range(PACK)]
+        for t in range(PACK):
+            s_ps = psum.tile([P, S], F32, name=f"s_ps{t}")
+            nc.tensor.matmul_mx(
+                out=s_ps[:],
+                lhsT=d_codes[:, t * P : (t + 1) * P].bitcast(FP8X4),
+                lhsT_scale=d_sc[:, t * P : (t + 1) * P],
+                rhs=x_codes[:].bitcast(FP8X4),
+                rhs_scale=x_sc[X_PLANE_ROW:P, :],
+                start=True,
+                stop=True,
+            )
+            if t == 0:
+                nc.scalar.activation(s_sb[t][:], s_ps[:], ACT.Copy, scale=0.0625)
+            else:
+                nc.vector.tensor_scalar_mul(s_sb[t][:], s_ps[:], 0.0625)
+
+        w_bf, w_codes, w_sc = {}, {}, {}
+
+        def round_w(m, slot):
+            w_bf[m] = sbuf([P, P, PACK], BF16, f"w_bf{m}", slot)
+            nc.vector.tensor_copy(
+                w_bf[m][:].rearrange("p (c i) t -> p c t i", i=4),
+                w_raw[:, :, m * P : (m + 1) * P].rearrange("p t (c i) -> p c t i", i=4),
+            )
+
+        def quantize_w(m):
+            w_codes[m] = sbuf([P, P], U32, f"w_codes{m}")
+            w_sc[m] = sbuf([P, P], U8, f"w_sc{m}")
+            nc.vector.quantize_mx(
+                out=w_codes[m][:].bitcast(FP8X4), scales=w_sc[m][:], in_=w_bf[m][:].rearrange("p c t -> p (c t)")
+            )
+
+        for t in range(PACK):
+            for lo in range(0, S, S // 2):
+                hi = lo + S // 2
+                nc.scalar.activation(s_n1[t][:, lo:hi], s_sb[t][:].indirect(list_slice(n1_l, lo, hi)), ACT.Copy)
+            nc.vector.tensor_tensor(st[t][:], s_sb[t][:], s_n1[t][:], ALU.max)
+            if t < PACK - 1:
+                round_w(t, f"s_n1{t}")
+                if t > 0:
+                    quantize_w(t - 1)
+        sl_th = sbuf([P, PACK], F32, "sl_th")
+        bias_t = sbuf([P, PACK], F32, "bias_t")
+        nc.gpsimd.tensor_tensor(sl_th[:], sl_t[:], th_t[:], ALU.mult)
+        nc.gpsimd.tensor_scalar(bias_t[:], sl_th[:], -1.0, 0.0, ALU.mult, ALU.add)
+
+        h_ps = [psum.tile([P, S], F32, name=f"h_ps{m}") for m in range(M_TILES)]
+        rl = [sbuf([P, S], F32, f"rl{m}") for m in range(M_TILES)]
+        ds = [sbuf([P, S], F32, f"ds{m}") for m in range(M_TILES)]
+        sg_slots = (None, f"s_n1{PACK - 1}", f"s_sb{PACK - 1}")
+        for c, (lo, hi) in enumerate(CHUNKS):
+            n = hi - lo
+            sg = sbuf([P, PACK, n], F32, f"sg{c}", sg_slots[c])
+            z_rows = sbuf([P, PACK, n], BF16, f"z_rows{c}")
+            z_bf = sbuf([P, n, PACK], BF16, f"z_bf{c}")
+            z_codes = sbuf([P, n], U32, f"z_codes{c}")
+            z_sc = sbuf([P, n], U8, f"z_sc{c}")
+            for t in range(PACK):
+                nc.scalar.activation(
+                    sg[:, t, :],
+                    st[t][:].indirect(list_slice(n2_l, lo, hi)),
+                    ACT.Sigmoid,
+                    bias=bias_t[:, t : t + 1],
+                    scale=sl_t[:, t : t + 1],
+                )
+                nc.vector.scalar_tensor_tensor(
+                    z_rows[:, t, :], sg[:, t, :], gn_t[:, t : t + 1], st[t][:, lo:hi], ALU.mult, ALU.mult
+                )
+            nc.vector.tensor_copy(
+                z_bf[:].rearrange("p (c i) t -> p c t i", i=4), z_rows[:].rearrange("p t (c i) -> p c t i", i=4)
+            )
+            if c == 0:
+                quantize_w(M_TILES - 2)
+            nc.vector.quantize_mx(out=z_codes[:].bitcast(FP8X4), scales=z_sc[:], in_=z_bf[:].rearrange("p c t -> p (c t)"))
+            if c == 0:
+                round_w(M_TILES - 1, "z_rows0")
+                quantize_w(M_TILES - 1)
+            for m in range(M_TILES):
+                nc.tensor.matmul_mx(
+                    out=h_ps[m][:, lo:hi],
+                    lhsT=w_codes[m][:].bitcast(FP8X4),
+                    lhsT_scale=w_sc[m][:],
+                    rhs=z_codes[:].bitcast(FP8X4),
+                    rhs_scale=z_sc[:],
+                    start=True,
+                    stop=True,
+                )
+                if c == 0 or m == 0:
+                    nc.vector.tensor_scalar_max(rl[m][:, lo:hi], h_ps[m][:, lo:hi], 0.0)
+                elif hi == S:
+                    rest = CHUNKS[0][1]
+                    nc.vector.tensor_scalar_max(rl[m][:, rest:S], h_ps[m][:, rest:S], 0.0)
+
+        def scatter(m, lo, hi):
+            nc.scalar.activation(ds[m][:].indirect(list_slice(n3_l, lo, hi)), rl[m][:, lo:hi], ACT.Copy)
+
+        first_hi = CHUNKS[0][1]
+        for m in range(M_TILES):
+            scatter(m, 0, first_hi)
+        for m in range(M_TILES):
+            if m == 0:
+                for lo, hi in CHUNKS[1:]:
+                    scatter(m, lo, hi)
+            else:
+                scatter(m, first_hi, S)
+            res = sbuf([P, S], F32, f"res{m}")
+            nc.vector.scalar_tensor_tensor(res[:], h_ps[m][:], -0.5, ds[m][:], ALU.mult, ALU.add)
+            nc.sync.dma_start(out=out[m * P : (m + 1) * P, :], in_=res[:])

@@ -78,6 +78,10 @@ def tile_picked_dwlehhsend_none_p_kernel(
             nc.sync.dma_start(out=col[:], in_=dram.rearrange("(p t) o -> p (t o)", t=PACK))
         nc.sync.dma_start(n3_l[:], n3)
 
+        warm = sbuf([P, 2], F32, "warm")
+        nc.vector.memset(warm[:, 0:1], 0.0)
+        nc.scalar.activation(warm[:, 1:2], warm[:, 0:1], ACT.Sigmoid)
+
         d_codes = sbuf([P, H], U32, "d_codes")
         d_sc = sbuf([P, H], U8, "d_sc")
         x_codes = sbuf([P, S], U32, "x_codes")

@@ -20,7 +20,7 @@ PACK = 4
 LIST_ROWS = 16
 X_PLANE_ROW = 4
 M_TILES = N // P
-CHUNKS = ((0, 64), (64, 128), (128, 256))
+CHUNKS = ((0, 128), (128, 256))
 
 
 def list_slice(offsets, lo, hi):
@@ -33,6 +33,7 @@ def tile_picked_dwlehhsend_none_p_kernel(
     nc = tc.nc
     with ExitStack() as ctx:
         keep = ctx.enter_context(tc.tile_pool(name="keep", bufs=1))
+        shared = ctx.enter_context(tc.tile_pool(name="shared", bufs=1))
         psum = ctx.enter_context(tc.psum_pool(name="psum", bufs=1))
 
         def sbuf(shape, dtype, name, slot=None):
@@ -43,7 +44,7 @@ def tile_picked_dwlehhsend_none_p_kernel(
         n1_l = sbuf([P, S // LIST_ROWS], U16, "n1_l")
         n2_l = sbuf([P, S // LIST_ROWS], U16, "n2_l")
         n3_l = sbuf([P, S // LIST_ROWS], U16, "n3_l")
-        d_tab = sbuf([P, G], I32, "d_tab")
+        d_tab = shared.tile([P, G], I32, name="d_tab", offset=0, align_bytes=64)
         x_tab = sbuf([P, T], I32, "x_tab")
         d_tab_sc = sbuf([P, G], U8, "d_tab_sc")
         x_tab_sc = sbuf([P, T], U8, "x_tab_sc")
@@ -83,15 +84,17 @@ def tile_picked_dwlehhsend_none_p_kernel(
         nc.scalar.activation(warm[:, 1:2], warm[:, 0:1], ACT.Sigmoid)
 
         d_codes = sbuf([P, H], U32, "d_codes")
-        d_sc = sbuf([P, H], U8, "d_sc")
-        x_codes = sbuf([P, S], U32, "x_codes")
-        x_sc = sbuf([P, S], U8, "x_sc")
+        d_sc = shared.tile([P, H], U8, name="d_sc", offset=0, align_bytes=64)
+        x_codes = sbuf([P, S], U32, "x_codes", "x_tab_sc")
+        x_sc = shared.tile([P, S], U8, name="x_sc", offset=H, align_bytes=64)
+        nc.vector.tensor_copy(d_codes[:].rearrange("p (t m) -> p m t", t=PACK), d_tab[:].bitcast(U32).indirect(ci_l[:]))
         nc.vector.tensor_copy(d_sc[:].rearrange("p (t m) -> p m t", t=PACK), d_tab_sc[:].indirect(ci_l[:]))
         nc.vector.tensor_copy(x_sc[:], x_tab_sc[:].indirect(offs_l[:]))
-        nc.vector.tensor_copy(d_codes[:].rearrange("p (t m) -> p m t", t=PACK), d_tab[:].bitcast(U32).indirect(ci_l[:]))
         nc.vector.tensor_copy(x_codes[:], x_tab[:].bitcast(U32).indirect(offs_l[:]))
 
-        s_sb = [sbuf([P, S], F32, f"s_sb{t}") for t in range(PACK)]
+        s_sb = [sbuf([P, 2 * S], F32, f"s_sb{t}") for t in range(PACK)]
+        for t in range(PACK):
+            nc.vector.memset(s_sb[t][:, S:], 0.0)
         s_n1 = [sbuf([P, S], F32, f"s_n1{t}") for t in range(PACK)]
         st = [sbuf([P, S], F32, f"st{t}") for t in range(PACK)]
         for t in range(PACK):
@@ -106,9 +109,9 @@ def tile_picked_dwlehhsend_none_p_kernel(
                 stop=True,
             )
             if t == 0:
-                nc.scalar.activation(s_sb[t][:], s_ps[:], ACT.Copy, scale=0.0625)
+                nc.scalar.activation(s_sb[t][:, :S], s_ps[:], ACT.Copy, scale=0.0625)
             else:
-                nc.vector.tensor_scalar_mul(s_sb[t][:], s_ps[:], 0.0625)
+                nc.vector.tensor_scalar_mul(s_sb[t][:, :S], s_ps[:], 0.0625)
 
         w_bf, w_codes, w_sc = {}, {}, {}
 
@@ -127,10 +130,8 @@ def tile_picked_dwlehhsend_none_p_kernel(
             )
 
         for t in range(PACK):
-            for lo in range(0, S, S // 2):
-                hi = lo + S // 2
-                nc.scalar.activation(s_n1[t][:, lo:hi], s_sb[t][:].indirect(list_slice(n1_l, lo, hi)), ACT.Copy)
-            nc.vector.tensor_tensor(st[t][:], s_sb[t][:], s_n1[t][:], ALU.max)
+            nc.scalar.activation(s_n1[t][:], s_sb[t][:].indirect(n1_l[:]), ACT.Copy)
+            nc.vector.tensor_tensor(st[t][:], s_sb[t][:, :S], s_n1[t][:], ALU.max)
             if t < PACK - 1:
                 round_w(t, f"s_n1{t}")
                 if t > 0:
@@ -194,11 +195,7 @@ def tile_picked_dwlehhsend_none_p_kernel(
         for m in range(M_TILES):
             scatter(m, 0, first_hi)
         for m in range(M_TILES):
-            if m == 0:
-                for lo, hi in CHUNKS[1:]:
-                    scatter(m, lo, hi)
-            else:
-                scatter(m, first_hi, S)
+            scatter(m, first_hi, S)
             res = sbuf([P, S], F32, f"res{m}")
             nc.vector.scalar_tensor_tensor(res[:], h_ps[m][:], -0.5, ds[m][:], ALU.mult, ALU.add)
             nc.sync.dma_start(out=out[m * P : (m + 1) * P, :], in_=res[:])

@@ -18,7 +18,6 @@ ACT = mybir.ActivationFunctionType
 P = 128
 PACK = 4
 LIST_ROWS = 16
-X_PLANE_ROW = 4
 M_TILES = N // P
 CHUNKS = ((0, 128), (128, 256))
 
@@ -33,7 +32,6 @@ def tile_picked_dwlehhsend_none_p_kernel(
     nc = tc.nc
     with ExitStack() as ctx:
         keep = ctx.enter_context(tc.tile_pool(name="keep", bufs=1))
-        shared = ctx.enter_context(tc.tile_pool(name="shared", bufs=1))
         psum = ctx.enter_context(tc.psum_pool(name="psum", bufs=1))
 
         def sbuf(shape, dtype, name, slot=None):
@@ -44,11 +42,10 @@ def tile_picked_dwlehhsend_none_p_kernel(
         n1_l = sbuf([P, S // LIST_ROWS], U16, "n1_l")
         n2_l = sbuf([P, S // LIST_ROWS], U16, "n2_l")
         n3_l = sbuf([P, S // LIST_ROWS], U16, "n3_l")
-        d_tab = shared.tile([P, G], I32, name="d_tab", offset=0, align_bytes=64)
+        d_tab = sbuf([P, G], I32, "d_tab")
         x_tab = sbuf([P, T], I32, "x_tab")
         d_tab_sc = sbuf([P, G], U8, "d_tab_sc")
         x_tab_sc = sbuf([P, T], U8, "x_tab_sc")
-        w_raw = sbuf([P, PACK, N], F32, "w_raw")
         sl_t = sbuf([P, PACK], F32, "sl_t")
         th_t = sbuf([P, PACK], F32, "th_t")
         gn_t = sbuf([P, PACK], F32, "gn_t")
@@ -56,41 +53,35 @@ def tile_picked_dwlehhsend_none_p_kernel(
         nc.vector.memset(d_tab_sc[:].bitcast(I32), 0)
         nc.vector.memset(x_tab_sc[:].bitcast(I32), 0)
 
-        def load_scales(eng, tab_sc, scales, row0, quads):
-            for q in quads:
-                eng.dma_start(
-                    out=tab_sc[32 * q + row0 : 32 * q + row0 + 4, :].bitcast(I32),
-                    in_=scales[0, 4 * q : 4 * q + 4, :].bitcast(I32),
-                )
-
         def words(dram):
             return dram[0].rearrange("p c r -> p (c r)").bitcast(I32)
 
-        load_scales(nc.scalar, d_tab_sc, d_scales, 0, range(4))
-        load_scales(nc.scalar, x_tab_sc, x_scales, X_PLANE_ROW, range(4))
-        nc.sync.dma_start(ci_l[:], ci)
-        nc.sync.dma_start(offs_l[:], offs)
+        for tab_sc, scales in ((d_tab_sc, d_scales), (x_tab_sc, x_scales)):
+            nc.scalar.dma_start(out=tab_sc[0:P:8, :].bitcast(I32), in_=scales[0].bitcast(I32))
+        for tile_l, dram in ((ci_l, ci), (offs_l, offs), (n1_l, n1), (n2_l, n2), (n3_l, n3)):
+            nc.sync.dma_start(tile_l[:], dram)
         nc.sync.dma_start(out=d_tab[:], in_=words(d_words))
         nc.sync.dma_start(out=x_tab[:], in_=words(x_words))
-        nc.sync.dma_start(n1_l[:], n1)
-        nc.sync.dma_start(n2_l[:], n2)
-        nc.sync.dma_start(out=w_raw[:], in_=w1.rearrange("(p t) n -> p t n", t=PACK))
         for col, dram in ((sl_t, sl), (th_t, th), (gn_t, gn)):
-            nc.sync.dma_start(out=col[:], in_=dram.rearrange("(p t) o -> p (t o)", t=PACK))
-        nc.sync.dma_start(n3_l[:], n3)
+            nc.gpsimd.dma_start(out=col[:], in_=dram.rearrange("(p t) o -> p (t o)", t=PACK))
 
         warm = sbuf([P, 2], F32, "warm")
         nc.vector.memset(warm[:, 0:1], 0.0)
         nc.scalar.activation(warm[:, 1:2], warm[:, 0:1], ACT.Sigmoid)
 
-        d_codes = sbuf([P, H], U32, "d_codes")
-        d_sc = shared.tile([P, H], U8, name="d_sc", offset=0, align_bytes=64)
-        x_codes = sbuf([P, S], U32, "x_codes", "x_tab_sc")
-        x_sc = shared.tile([P, S], U8, name="x_sc", offset=H, align_bytes=64)
+        picked_sc = sbuf([P, H + S], U8, "picked_sc")
+        planes = sbuf([P, H + S], U8, "planes")
+        nc.vector.memset(planes[:].bitcast(I32), 0)
+        nc.vector.tensor_copy(picked_sc[:, :H].rearrange("p (t m) -> p m t", t=PACK), d_tab_sc[:].indirect(ci_l[:]))
+        nc.vector.tensor_copy(picked_sc[:, H:], x_tab_sc[:].indirect(offs_l[:]))
+        for i in range(4):
+            nc.scalar.dma_start(out=planes[i:P:32, :].bitcast(I32), in_=picked_sc[8 * i : P : 32, :].bitcast(I32))
+        d_codes = sbuf([P, H], U32, "d_codes", "x_tab_sc")
+        x_codes = sbuf([P, S], U32, "x_codes")
         nc.vector.tensor_copy(d_codes[:].rearrange("p (t m) -> p m t", t=PACK), d_tab[:].bitcast(U32).indirect(ci_l[:]))
-        nc.vector.tensor_copy(d_sc[:].rearrange("p (t m) -> p m t", t=PACK), d_tab_sc[:].indirect(ci_l[:]))
-        nc.vector.tensor_copy(x_sc[:], x_tab_sc[:].indirect(offs_l[:]))
         nc.vector.tensor_copy(x_codes[:], x_tab[:].bitcast(U32).indirect(offs_l[:]))
+        w_raw = sbuf([P, PACK, N], F32, "w_raw", "d_tab")
+        nc.sync.dma_start(out=w_raw[:], in_=w1.rearrange("(p t) n -> p t n", t=PACK))
 
         s_sb = [sbuf([P, 2 * S], F32, f"s_sb{t}") for t in range(PACK)]
         for t in range(PACK):
@@ -102,9 +93,9 @@ def tile_picked_dwlehhsend_none_p_kernel(
             nc.tensor.matmul_mx(
                 out=s_ps[:],
                 lhsT=d_codes[:, t * P : (t + 1) * P].bitcast(FP8X4),
-                lhsT_scale=d_sc[:, t * P : (t + 1) * P],
+                lhsT_scale=planes[:, t * P : (t + 1) * P],
                 rhs=x_codes[:].bitcast(FP8X4),
-                rhs_scale=x_sc[X_PLANE_ROW:P, :],
+                rhs_scale=planes[:, H:],
                 start=True,
                 stop=True,
             )
@@ -132,10 +123,10 @@ def tile_picked_dwlehhsend_none_p_kernel(
         for t in range(PACK):
             nc.scalar.activation(s_n1[t][:], s_sb[t][:].indirect(n1_l[:]), ACT.Copy)
             nc.vector.tensor_tensor(st[t][:], s_sb[t][:, :S], s_n1[t][:], ALU.max)
-            if t < PACK - 1:
-                round_w(t, f"s_n1{t}")
-                if t > 0:
-                    quantize_w(t - 1)
+            if t >= 1:
+                round_w(t - 1, f"s_sb{t}")
+            if t >= 2:
+                quantize_w(t - 2)
         sl_th = sbuf([P, PACK], F32, "sl_th")
         bias_t = sbuf([P, PACK], F32, "bias_t")
         nc.gpsimd.tensor_tensor(sl_th[:], sl_t[:], th_t[:], ALU.mult)

from contextlib import ExitStack

import concourse.mybir as mybir

K, T, S, N, G, H = 512, 2048, 256, 512, 2048, 512
FLOPS = 2 * K * H * S + 2 * H * N * S

F32 = mybir.dt.float32
BF16 = mybir.dt.bfloat16
I32 = mybir.dt.int32
U32 = mybir.dt.uint32
U16 = mybir.dt.uint16
U8 = mybir.dt.uint8
FP8X4 = mybir.dt.float8_e4m3fn_x4
ALU = mybir.AluOpType
ACT = mybir.ActivationFunctionType

P = 128
PACK = 4
LIST_ROWS = 16
M_TILES = N // P
CHUNKS = ((0, 128), (128, 256))


def list_slice(offsets, lo, hi):
    return offsets[:, lo // LIST_ROWS : hi // LIST_ROWS]


def tile_picked_dwlehhsend_none_p_kernel(
    tc, x_words, x_scales, d_words, d_scales, sl, th, gn, w1, offs, ci, n1, n2, n3, out
):
    nc = tc.nc
    with ExitStack() as ctx:
        keep = ctx.enter_context(tc.tile_pool(name="keep", bufs=1))
        psum = ctx.enter_context(tc.psum_pool(name="psum", bufs=1))

        def sbuf(shape, dtype, name, slot=None):
            return keep.tile(shape, dtype, name=name, tag=slot or name, align_bytes=64)

        ci_l = sbuf([P, H // LIST_ROWS], U16, "ci_l")
        offs_l = sbuf([P, S // LIST_ROWS], U16, "offs_l")
        n1_l = sbuf([P, S // LIST_ROWS], U16, "n1_l")
        n2_l = sbuf([P, S // LIST_ROWS], U16, "n2_l")
        n3_l = sbuf([P, S // LIST_ROWS], U16, "n3_l")
        d_tab = sbuf([P, G], I32, "d_tab")
        x_tab = sbuf([P, T], I32, "x_tab")
        d_tab_sc = sbuf([P, G], U8, "d_tab_sc")
        x_tab_sc = sbuf([P, T], U8, "x_tab_sc")
        sl_t = sbuf([P, PACK], F32, "sl_t")
        th_t = sbuf([P, PACK], F32, "th_t")
        gn_t = sbuf([P, PACK], F32, "gn_t")

        nc.vector.memset(d_tab_sc[:].bitcast(I32), 0)
        nc.vector.memset(x_tab_sc[:].bitcast(I32), 0)

        def words(dram):
            return dram[0].rearrange("p c r -> p (c r)").bitcast(I32)

        for tab_sc, scales in ((d_tab_sc, d_scales), (x_tab_sc, x_scales)):
            nc.scalar.dma_start(out=tab_sc[0:P:8, :].bitcast(I32), in_=scales[0].bitcast(I32))
        for tile_l, dram in ((ci_l, ci), (offs_l, offs), (n1_l, n1), (n2_l, n2), (n3_l, n3)):
            nc.sync.dma_start(tile_l[:], dram)
        nc.sync.dma_start(out=d_tab[:], in_=words(d_words))
        nc.sync.dma_start(out=x_tab[:], in_=words(x_words))
        for col, dram in ((sl_t, sl), (th_t, th), (gn_t, gn)):
            nc.gpsimd.dma_start(out=col[:], in_=dram.rearrange("(p t) o -> p (t o)", t=PACK))

        warm = sbuf([P, 2], F32, "warm")
        nc.vector.memset(warm[:, 0:1], 0.0)
        nc.scalar.activation(warm[:, 1:2], warm[:, 0:1], ACT.Sigmoid)

        picked_sc = sbuf([P, H + S], U8, "picked_sc")
        planes = sbuf([P, H + S], U8, "planes")
        nc.vector.memset(planes[:].bitcast(I32), 0)
        nc.vector.tensor_copy(picked_sc[:, :H].rearrange("p (t m) -> p m t", t=PACK), d_tab_sc[:].indirect(ci_l[:]))
        nc.vector.tensor_copy(picked_sc[:, H:], x_tab_sc[:].indirect(offs_l[:]))
        for i in range(4):
            nc.scalar.dma_start(out=planes[i:P:32, :].bitcast(I32), in_=picked_sc[8 * i : P : 32, :].bitcast(I32))
        d_codes = sbuf([P, H], U32, "d_codes", "x_tab_sc")
        x_codes = sbuf([P, S], U32, "x_codes")
        nc.vector.tensor_copy(d_codes[:].rearrange("p (t m) -> p m t", t=PACK), d_tab[:].bitcast(U32).indirect(ci_l[:]))
        nc.vector.tensor_copy(x_codes[:], x_tab[:].bitcast(U32).indirect(offs_l[:]))
        w_raw = sbuf([P, PACK, N], F32, "w_raw", "d_tab")
        nc.sync.dma_start(out=w_raw[:], in_=w1.rearrange("(p t) n -> p t n", t=PACK))

        s_sb = [sbuf([P, 2 * S], F32, f"s_sb{t}") for t in range(PACK)]
        for t in range(PACK):
            nc.vector.memset(s_sb[t][:, S:], 0.0)
        s_n1 = [sbuf([P, S], F32, f"s_n1{t}") for t in range(PACK)]
        st = [sbuf([P, S], F32, f"st{t}") for t in range(PACK)]
        for t in range(PACK):
            s_ps = psum.tile([P, S], F32, name=f"s_ps{t}")
            nc.tensor.matmul_mx(
                out=s_ps[:],
                lhsT=d_codes[:, t * P : (t + 1) * P].bitcast(FP8X4),
                lhsT_scale=planes[:, t * P : (t + 1) * P],
                rhs=x_codes[:].bitcast(FP8X4),
                rhs_scale=planes[:, H:],
                start=True,
                stop=True,
            )
            if t == 0:
                nc.scalar.activation(s_sb[t][:, :S], s_ps[:], ACT.Copy, scale=0.0625)
            else:
                nc.vector.tensor_scalar_mul(s_sb[t][:, :S], s_ps[:], 0.0625)

        w_bf, w_codes, w_sc = {}, {}, {}

        def round_w(m, slot):
            w_bf[m] = sbuf([P, P, PACK], BF16, f"w_bf{m}", slot)
            nc.vector.tensor_copy(
                w_bf[m][:].rearrange("p (c i) t -> p c t i", i=4),
                w_raw[:, :, m * P : (m + 1) * P].rearrange("p t (c i) -> p c t i", i=4),
            )

        def quantize_w(m):
            w_codes[m] = sbuf([P, P], U32, f"w_codes{m}")
            w_sc[m] = sbuf([P, P], U8, f"w_sc{m}")
            nc.vector.quantize_mx(
                out=w_codes[m][:].bitcast(FP8X4), scales=w_sc[m][:], in_=w_bf[m][:].rearrange("p c t -> p (c t)")
            )

        for t in range(PACK):
            nc.scalar.activation(s_n1[t][:], s_sb[t][:].indirect(n1_l[:]), ACT.Copy)
            nc.vector.tensor_tensor(st[t][:], s_sb[t][:, :S], s_n1[t][:], ALU.max)
            if t >= 1:
                round_w(t - 1, f"s_sb{t}")
            if t >= 2:
                quantize_w(t - 2)
        sl_th = sbuf([P, PACK], F32, "sl_th")
        bias_t = sbuf([P, PACK], F32, "bias_t")
        nc.gpsimd.tensor_tensor(sl_th[:], sl_t[:], th_t[:], ALU.mult)
        nc.gpsimd.tensor_scalar(bias_t[:], sl_th[:], -1.0, 0.0, ALU.mult, ALU.add)

        h_ps = [psum.tile([P, S], F32, name=f"h_ps{m}") for m in range(M_TILES)]
        rl = [sbuf([P, S], F32, f"rl{m}") for m in range(M_TILES)]
        ds = [sbuf([P, S], F32, f"ds{m}") for m in range(M_TILES)]
        sg_slots = (None, f"s_n1{PACK - 1}", f"s_sb{PACK - 1}")
        for c, (lo, hi) in enumerate(CHUNKS):
            n = hi - lo
            sg = sbuf([P, PACK, n], F32, f"sg{c}", sg_slots[c])
            z_rows = sbuf([P, PACK, n], BF16, f"z_rows{c}")
            z_bf = sbuf([P, n, PACK], BF16, f"z_bf{c}")
            z_codes = sbuf([P, n], U32, f"z_codes{c}")
            z_sc = sbuf([P, n], U8, f"z_sc{c}")
            for t in range(PACK):
                nc.scalar.activation(
                    sg[:, t, :],
                    st[t][:].indirect(list_slice(n2_l, lo, hi)),
                    ACT.Sigmoid,
                    bias=bias_t[:, t : t + 1],
                    scale=sl_t[:, t : t + 1],
                )
                nc.vector.scalar_tensor_tensor(
                    z_rows[:, t, :], sg[:, t, :], gn_t[:, t : t + 1], st[t][:, lo:hi], ALU.mult, ALU.mult
                )
            nc.vector.tensor_copy(
                z_bf[:].rearrange("p (c i) t -> p c t i", i=4), z_rows[:].rearrange("p t (c i) -> p c t i", i=4)
            )
            if c == 0:
                quantize_w(M_TILES - 2)
            nc.vector.quantize_mx(out=z_codes[:].bitcast(FP8X4), scales=z_sc[:], in_=z_bf[:].rearrange("p c t -> p (c t)"))
            if c == 0:
                round_w(M_TILES - 1, "z_rows0")
                quantize_w(M_TILES - 1)
            for m in range(M_TILES):
                nc.tensor.matmul_mx(
                    out=h_ps[m][:, lo:hi],
                    lhsT=w_codes[m][:].bitcast(FP8X4),
                    lhsT_scale=w_sc[m][:],
                    rhs=z_codes[:].bitcast(FP8X4),
                    rhs_scale=z_sc[:],
                    start=True,
                    stop=True,
                )
                if c == 0 or m == 0:
                    nc.vector.tensor_scalar_max(rl[m][:, lo:hi], h_ps[m][:, lo:hi], 0.0)
                elif hi == S:
                    rest = CHUNKS[0][1]
                    nc.vector.tensor_scalar_max(rl[m][:, rest:S], h_ps[m][:, rest:S], 0.0)

        def scatter(m, lo, hi):
            nc.scalar.activation(ds[m][:].indirect(list_slice(n3_l, lo, hi)), rl[m][:, lo:hi], ACT.Copy)

        first_hi = CHUNKS[0][1]
        for m in range(M_TILES):
            scatter(m, 0, first_hi)
        for m in range(M_TILES):
            scatter(m, first_hi, S)
            res = sbuf([P, S], F32, f"res{m}")
            nc.vector.scalar_tensor_tensor(res[:], h_ps[m][:], -0.5, ds[m][:], ALU.mult, ALU.add)
            nc.sync.dma_start(out=out[m * P : (m + 1) * P, :], in_=res[:])
